import numpy as np
import ml_dtypes


def mxq(x, axis, fmt="e4m3"):
    dtype, down = {"e4m3": (ml_dtypes.float8_e4m3fn, 7), "e5m2": (ml_dtypes.float8_e5m2, 14)}[fmt]
    v = np.moveaxis(np.asarray(x, np.float32).astype(ml_dtypes.bfloat16).astype(np.float64), axis, -1)
    blocks = v.reshape(v.shape[:-1] + (-1, 32))
    amax = np.abs(blocks).max(-1, keepdims=True)
    byte = np.maximum(np.where(amax > 0, np.frexp(amax)[1] - 1 + 127, 0) - down, 1)
    scale = np.exp2(byte - 127.0)
    codes = (blocks / scale).astype(np.float32).astype(dtype).astype(np.float64)
    return np.moveaxis((codes * scale).reshape(v.shape), -1, axis)


WIDE = False


def mx_kscale(k):
    if not WIDE:
        return np.ones(k)
    levels = np.array([10, -10, 5, -5, 0])
    if k % 512:
        return np.exp2(np.random.permutation(np.resize(levels, k // 32))).repeat(32)
    a = np.empty((k // 512, 16))
    for p in range(k // 512):
        a[p, :8] = np.random.permutation(np.resize(levels, 8))
        for g in range(8):
            far = levels[np.abs(levels - a[p, g]) >= 10]
            a[p, g + 8] = far[np.random.randint(len(far))]
    return np.exp2(a.ravel()).repeat(32)


def f64(x):
    return np.asarray(x).astype(np.float64)


def striped8(idx):
    return np.concatenate([x.reshape(-1, 16).T for x in idx]).astype(np.uint16)


def runs(offs, k):
    lists = np.stack([offs[16 * r : 16 * r + 16].T.reshape(-1) for r in range(8)]).astype(np.int64)
    return lists[np.arange(k) % 512 // 64]


def pack_weight(w):
    k, n = w.shape
    w = f64(np.asarray(w, np.float32).astype(ml_dtypes.bfloat16)).reshape(k // 32, 32, n)
    amax = np.abs(w).max(1)
    byte = np.clip(np.where(amax > 0, np.frexp(amax)[1] - 1 + 127 - 7, 1), 1, 254)
    scaled = (w * np.exp2(127.0 - byte)[:, None, :]).reshape(k, n).astype(np.float32)
    words = np.ascontiguousarray(scaled.reshape(k // 512, 128, 4, n).transpose(0, 1, 3, 2)).astype(ml_dtypes.float8_e4m3fn).view(np.uint8)
    return words, np.ascontiguousarray(byte.astype(np.uint8).reshape(k // 512, 16, n))


def unpack_weight(words, scales):
    g, p, n, _ = words.shape
    vals = np.ascontiguousarray(words).view(ml_dtypes.float8_e4m3fn).astype(np.float64) * np.repeat(np.exp2(scales.astype(np.float64) - 127.0), 8, axis=1)[..., None]
    return vals.transpose(0, 1, 3, 2).reshape(g * 512, n)


E2M1 = np.array([0.0, 0.5, 1.0, 1.5, 2.0, 3.0, 4.0, 6.0, -0.0, -0.5, -1.0, -1.5, -2.0, -3.0, -4.0, -6.0])


def pack_fp4(w):
    k, n = w.shape
    w = f64(np.asarray(w, np.float32).astype(ml_dtypes.bfloat16)).reshape(k // 32, 32, n)
    amax = np.abs(w).max(1)
    mant, ex = np.frexp(amax / 6.0)
    byte = np.clip(np.where(amax > 0, np.where(mant > 0.5, ex, ex - 1) + 127, 1), 1, 254)
    scaled = (w * np.exp2(127.0 - byte)[:, None, :]).reshape(k, n).astype(np.float32)
    c = np.ascontiguousarray(scaled.reshape(k // 512, 128, 4, n).transpose(0, 1, 3, 2)).astype(ml_dtypes.float4_e2m1fn).view(np.uint8) & 0xF
    words = (c[..., 0::2] | (c[..., 1::2] << 4)).reshape(k // 512, 128, 2 * n)
    return np.ascontiguousarray(words), np.ascontiguousarray(byte.astype(np.uint8).reshape(k // 512, 16, n))


def unpack_fp4(words, scales):
    g, _, n = scales.shape
    words = np.ascontiguousarray(words).reshape(g, 128, n, 2)
    nib = np.empty((g, 128, n, 4), np.uint8)
    nib[..., 0::2] = words & 0xF
    nib[..., 1::2] = words >> 4
    vals = E2M1[nib] * np.repeat(np.exp2(scales.astype(np.float64) - 127.0), 8, axis=1)[..., None]
    return vals.transpose(0, 1, 3, 2).reshape(g * 512, n)


def planes(y):
    n, m = y.shape
    v = y.astype(np.float32).astype(ml_dtypes.bfloat16).astype(np.float64).reshape(n // 32, 32, m)
    top = np.abs(v).max(1)
    byte = np.clip(np.where(top > 0, np.frexp(top)[1] - 1 + 127 - 7, 1), 1, 254)
    codes = (v * np.exp2(127.0 - byte)[:, None, :]).reshape(n, m).astype(np.float32).astype(ml_dtypes.float8_e4m3fn).view(np.uint8)
    words = codes.reshape(n // 512, 128, 4, m).transpose(0, 1, 3, 2)
    return np.ascontiguousarray(words), np.ascontiguousarray(byte.astype(np.uint8).reshape(n // 512, 16, m))


K, T, S, N, H = 512, 2048, 512, 512, 512


def setup_inputs():
    n = np.random.standard_normal
    s = mx_kscale(K)[:, None]
    u = mx_kscale(H)
    packed_xT = pack_weight(n((K, T)) * s)
    packed_w1 = pack_fp4(n((K, H)) / np.sqrt(K) / s)
    packed_w2 = pack_fp4(n((H, N)) / np.sqrt(H) / u[:, None])
    return {
        "x_words": packed_xT[0],
        "x_scales": packed_xT[1],
        "w1_words": packed_w1[0],
        "w1_scales": packed_w1[1],
        "gn": (np.random.uniform(0.5, 1.5, (H, 1)) * u[:, None]).astype(np.float32),
        "w2_words": packed_w2[0],
        "w2_scales": packed_w2[1],
        "offs": striped8(np.random.randint(0, T, (8, S))),
        "n1": striped8(np.stack([np.random.permutation(S) for _ in range(8)])),
        "n2": striped8(np.stack([np.random.permutation(S) for _ in range(8)])),
        "n3": striped8(np.stack([np.random.permutation(S) for _ in range(8)])),
    }


def reference(x_words, x_scales, w1_words, w1_scales, gn, w2_words, w2_scales, offs, n1, n2, n3):
    xq = unpack_weight(x_words, x_scales)[np.arange(K)[:, None], runs(offs, K)]
    y = unpack_fp4(w1_words, w1_scales).T @ xq
    z = f64(gn) * (y[np.arange(H)[:, None], runs(n1, H)] + 0.75 * (y[np.arange(H)[:, None], runs(n2, H)]))
    h = unpack_fp4(w2_words, w2_scales).T @ mxq(z, 0, "e4m3")
    st = h - (h[np.arange(N)[:, None], runs(n3, N)])
    out_0 = st - (0.5 * (st[np.arange(N)[:, None], runs(n3, N)]))
    return (out_0,) + planes(out_0)

@@ -1,0 +1,208 @@
+from contextlib import ExitStack
+
+import concourse.mybir as mybir
+
+K, T, S, N, H = 512, 2048, 512, 512, 512
+FLOPS = 2 * K * H * S + 2 * H * N * S
+
+F32 = mybir.dt.float32
+BF16 = mybir.dt.bfloat16
+I32 = mybir.dt.int32
+U32 = mybir.dt.uint32
+U16 = mybir.dt.uint16
+U8 = mybir.dt.uint8
+FP8X4 = mybir.dt.float8_e4m3fn_x4
+FP4X4 = mybir.dt.float4_e2m1fn_x4
+COPY = mybir.ActivationFunctionType.Copy
+MULT = mybir.AluOpType.mult
+ADD = mybir.AluOpType.add
+SUB = mybir.AluOpType.subtract
+
+P = 128
+PACK = 4
+HALF = S // 2
+CHUNKS = ((0, 256), (256, 128), (384, 128))
+
+
+def entries(lists, start, width):
+    return lists[:, start // 16 : (start + width) // 16]
+
+
+def interleave(engine_copy, dst, src):
+    engine_copy(
+        dst[:].rearrange("p (c i) t -> p c t i", i=4),
+        src[:].rearrange("p t (c i) -> p c t i", i=4),
+    )
+
+
+def tile_picked_hashsumtwice_none_po_kernel(
+    tc, x_words, x_scales, w1_words, w1_scales, gn, w2_words, w2_scales, offs, n1, n2, n3, out_0, out_1, out_2
+):
+    nc = tc.nc
+    with ExitStack() as ctx:
+        keep = ctx.enter_context(tc.tile_pool(name="keep", bufs=1))
+        psum = ctx.enter_context(tc.psum_pool(name="psum", bufs=1))
+
+        def sb(shape, dtype, name):
+            return keep.tile(shape, dtype, name=name, align_bytes=64)
+
+        def bank(index, shape, name):
+            return psum.tile(shape, F32, name=name, tag="bank%d" % index)
+
+        offs_t = keep.tile([P, S // 16], U16, name="offs_t")
+        n1_t = keep.tile([P, S // 16], U16, name="n1_t")
+        n2_t = keep.tile([P, S // 16], U16, name="n2_t")
+        n3_t = keep.tile([P, S // 16], U16, name="n3_t")
+        table_words = sb([P, T], U32, "table_words")
+        nc.sync.dma_start(offs_t[:], offs)
+        nc.sync.dma_start(n2_t[:], n2)
+        nc.sync.dma_start(table_words[:].bitcast(I32), x_words[0].rearrange("p n t -> p (n t)").bitcast(I32))
+        nc.sync.dma_start(n1_t[:], n1)
+        nc.sync.dma_start(n3_t[:], n3)
+
+        def load_words(words, name, queue):
+            raw_words = sb([P, 2 * H], U8, name + "_raw_words")
+            queue.dma_start(raw_words[:].bitcast(I32), words[0].bitcast(I32))
+            return raw_words
+
+        def load_scales(scales, name, clearer, queue):
+            raw_scales = sb([P, H], U8, name + "_raw_scales")
+            clearer.memset(raw_scales[:].bitcast(I32), 0)
+            for q in range(4):
+                queue.dma_start(
+                    raw_scales[32 * q : 32 * q + 4, :].bitcast(I32), scales[0, 4 * q : 4 * q + 4, :].bitcast(I32)
+                )
+            return raw_scales
+
+        def deal_weight(raw_words, raw_scales, name):
+            words = sb([P, PACK, 2 * P], U8, name + "_words")
+            scales = sb([P, PACK, P], U8, name + "_scales")
+            nc.vector.tensor_copy(
+                words[:].rearrange("p t (g m b) -> p g t m b", m=8, b=2),
+                raw_words[:].rearrange("p (g m t b) -> p g t m b", m=8, t=PACK, b=2),
+            )
+            nc.vector.tensor_copy(
+                scales[:].rearrange("p t (g m) -> p g t m", m=16),
+                raw_scales[:].rearrange("p (g m t) -> p g t m", m=16, t=PACK),
+            )
+            return words, scales
+
+        w1_raw_words = load_words(w1_words, "w1", nc.scalar)
+        table_scales = sb([P, T], U8, "table_scales")
+        nc.vector.memset(table_scales[:].bitcast(I32), 0)
+        nc.scalar.dma_start(table_scales[0:P:8, :].bitcast(I32), x_scales[0].bitcast(I32))
+        w1_raw = (w1_raw_words, load_scales(w1_scales, "w1", nc.vector, nc.scalar))
+
+        gain = sb([P, PACK], F32, "gain")
+        w2_raw_words = load_words(w2_words, "w2", nc.gpsimd)
+        nc.gpsimd.dma_start(gain[:], gn.rearrange("(p t) o -> p (t o)", t=PACK))
+        w2_raw = (w2_raw_words, load_scales(w2_scales, "w2", nc.gpsimd, nc.gpsimd))
+
+        x_scale = sb([P, S], U8, "x_scale")
+        nc.vector.memset(x_scale[:].bitcast(I32), 0)
+        picked_rows = sb([P, S], U8, "picked_rows")
+        nc.vector.tensor_copy(picked_rows[:], table_scales[:].indirect(offs_t[:]))
+        for j in range(4):
+            nc.sync.dma_start(x_scale[j:P:32, :].bitcast(I32), picked_rows[8 * j : P : 32, :].bitcast(I32))
+
+        w1q, w1s = deal_weight(*w1_raw, "w1")
+
+        x_codes = sb([P, S], U32, "x_codes")
+        for h0 in (0, HALF):
+            nc.vector.tensor_copy(x_codes[:, h0 : h0 + HALF], table_words[:].indirect(entries(offs_t, h0, HALF)))
+
+        w2q, w2s = deal_weight(*w2_raw, "w2")
+
+        def product(acc, wq, ws, t, codes, scales):
+            nc.tensor.matmul_mx(
+                out=acc,
+                lhsT=wq[:, t, :].bitcast(FP4X4),
+                lhsT_scale=ws[:, t, :],
+                rhs=codes.bitcast(FP8X4),
+                rhs_scale=scales,
+                start=True,
+                stop=True,
+            )
+
+        gy = [sb([P, S], F32, "gy%d" % t) for t in range(PACK)]
+        pieces = [(0, 0, HALF), (0, HALF, HALF)] + [(t, 0, S) for t in range(1, PACK)]
+        for b, (t, c0, n) in enumerate(pieces):
+            acc = bank(b, [P, n], "y_acc%d" % b)
+            product(acc[:], w1q, w1s, t, x_codes[:, c0 : c0 + n], x_scale[:, c0 : c0 + n])
+            nc.scalar.activation(gy[t][:, c0 : c0 + n], acc[:], COPY, scale=gain[:, t : t + 1])
+
+        hw = [sb([P, S], F32, "hw%d" % t) for t in range(PACK)]
+        hp = [sb([P, S], F32, "hp%d" % t) for t in range(PACK)]
+        h_banks = ((5, 5, 6, 6), (7, 7, 7, 7), (0, 1, 2, 3))
+        last = len(CHUNKS) - 1
+
+        def second_product(c, zb):
+            c0, n = CHUNKS[c]
+            zq = sb([P, n], U32, "zq%d" % c)
+            zs = sb([P, n], U8, "zs%d" % c)
+            nc.vector.quantize_mx(out=zq[:].bitcast(FP8X4), scales=zs[:], in_=zb[:].rearrange("p c t -> p (c t)"))
+            accs = {}
+            for t in range(PACK):
+                b = h_banks[c][t]
+                shared = h_banks[c].count(b)
+                if b not in accs:
+                    accs[b] = bank(b, [P, shared, n], "h_acc%d_%d" % (c, b))
+                product(accs[b][:, t % shared, :], w2q, w2s, t, zq[:], zs[:])
+            for dst in (hw, hp):
+                for t in range(PACK):
+                    b = h_banks[c][t]
+                    shared = h_banks[c].count(b)
+                    nc.scalar.activation(dst[t][:, c0 : c0 + n], accs[b][:, t % shared, :], COPY, scale=0.5)
+
+        waiting = None
+        for c, (c0, n) in enumerate(CHUNKS):
+            part = sb([P, PACK, n], F32, "part%d" % c)
+            z = sb([P, PACK, n], F32, "z%d" % c)
+            zb = sb([P, n, PACK], BF16, "zb%d" % c)
+            for t in range(PACK + 1):
+                if t < PACK:
+                    nc.vector.tensor_scalar(part[:, t, :], gy[t][:].indirect(entries(n2_t, c0, n)), 0.75, 0.0, MULT, ADD)
+                if t > 0:
+                    nc.vector.tensor_tensor(z[:, t - 1, :], gy[t - 1][:].indirect(entries(n1_t, c0, n)), part[:, t - 1, :], ADD)
+            if waiting is not None:
+                second_product(*waiting)
+            interleave(nc.vector.tensor_copy if c == last else nc.scalar.copy, zb, z)
+            waiting = (c, zb)
+        second_product(*waiting)
+
+        w = [sb([P, S], F32, "w%d" % t) for t in range(PACK)]
+        d = [sb([P, S], F32, "d%d" % t) for t in range(PACK)]
+        for t in range(PACK):
+            for h0 in (0, HALF):
+                nc.vector.tensor_tensor(
+                    w[t][:, h0 : h0 + HALF], hw[t][:].indirect(entries(n3_t, h0, HALF)), hp[t][:, h0 : h0 + HALF], SUB
+                )
+            nc.scalar.activation(d[t][:], w[t][:], COPY, scale=2.0)
+
+        out_rows = out_0.rearrange("(p t) j -> p t j", t=PACK)
+        out_words = out_1[0].rearrange("p n t -> p (n t)").bitcast(I32)
+        o_scale = sb([P, S], U8, "o_scale")
+
+        def planes(c, ob):
+            c0, n = CHUNKS[c]
+            oq = sb([P, n], U32, "oq%d" % c)
+            nc.vector.quantize_mx(
+                out=oq[:].bitcast(FP8X4), scales=o_scale[:, c0 : c0 + n], in_=ob[:].rearrange("p c t -> p (c t)")
+            )
+            nc.sync.dma_start(out_words[:, c0 : c0 + n], oq[:].bitcast(I32))
+
+        waiting = None
+        for c, (c0, n) in enumerate(CHUNKS):
+            o = sb([P, PACK, n], F32, "o%d" % c)
+            ob = sb([P, n, PACK], BF16, "ob%d" % c)
+            for t in range(PACK):
+                nc.vector.tensor_tensor(o[:, t, :], w[t][:].indirect(entries(n3_t, c0, n)), d[t][:, c0 : c0 + n], SUB)
+            nc.sync.dma_start(out_rows[:, :, c0 : c0 + n], o[:])
+            if waiting is not None:
+                planes(*waiting)
+            interleave(nc.vector.tensor_copy if c == last else nc.scalar.copy, ob, o)
+            waiting = (c, ob)
+        planes(*waiting)
+        for q in range(4):
+            queue = nc.scalar if q % 2 == 0 else nc.sync
+            queue.dma_start(out_2[0, 4 * q : 4 * q + 4, :].bitcast(I32), o_scale[32 * q : 32 * q + 4, :].bitcast(I32))

@@ -21,7 +21,7 @@ SUB = mybir.AluOpType.subtract
 P = 128
 PACK = 4
 HALF = S // 2
-CHUNKS = ((0, 256), (256, 128), (384, 128))
+CHUNKS = ((0, HALF), (HALF, HALF))
 
 
 def entries(lists, start, width):
@@ -41,6 +41,7 @@ def tile_picked_hashsumtwice_none_po_kernel(
     nc = tc.nc
     with ExitStack() as ctx:
         keep = ctx.enter_context(tc.tile_pool(name="keep", bufs=1))
+        ring = ctx.enter_context(tc.tile_pool(name="ring", bufs=3))
         psum = ctx.enter_context(tc.psum_pool(name="psum", bufs=1))
 
         def sb(shape, dtype, name):
@@ -54,49 +55,44 @@ def tile_picked_hashsumtwice_none_po_kernel(
         n2_t = keep.tile([P, S // 16], U16, name="n2_t")
         n3_t = keep.tile([P, S // 16], U16, name="n3_t")
         table_words = sb([P, T], U32, "table_words")
-        nc.sync.dma_start(offs_t[:], offs)
-        nc.sync.dma_start(n2_t[:], n2)
-        nc.sync.dma_start(table_words[:].bitcast(I32), x_words[0].rearrange("p n t -> p (n t)").bitcast(I32))
-        nc.sync.dma_start(n1_t[:], n1)
-        nc.sync.dma_start(n3_t[:], n3)
+        table_scales = sb([P, T], U8, "table_scales")
+        gain = sb([P, PACK], F32, "gain")
 
-        def load_words(words, name, queue):
-            raw_words = sb([P, 2 * H], U8, name + "_raw_words")
-            queue.dma_start(raw_words[:].bitcast(I32), words[0].bitcast(I32))
-            return raw_words
+        raw_scales = sb([P, H], U8, "raw_scales")
+        w1_raw_words = sb([P, 2 * H], U8, "w1_raw_words")
+        w2_raw_words = sb([P, 2 * H], U8, "w2_raw_words")
 
-        def load_scales(scales, name, clearer, queue):
-            raw_scales = sb([P, H], U8, name + "_raw_scales")
-            clearer.memset(raw_scales[:].bitcast(I32), 0)
-            for q in range(4):
-                queue.dma_start(
-                    raw_scales[32 * q : 32 * q + 4, :].bitcast(I32), scales[0, 4 * q : 4 * q + 4, :].bitcast(I32)
-                )
-            return raw_scales
+        def load_scales(scales, j, queue):
+            rows = scales[0].bitcast(I32).rearrange("(q j) c -> j q c", j=4)[j]
+            queue.dma_start(raw_scales[j:P:4, :].bitcast(I32), rows.unsqueeze(1).to_broadcast([4, 8, H // 4]))
 
-        def deal_weight(raw_words, raw_scales, name):
-            words = sb([P, PACK, 2 * P], U8, name + "_words")
-            scales = sb([P, PACK, P], U8, name + "_scales")
+        def deal_words(raw_words, name):
+            words = sb([P, PACK, 2 * P], U8, name)
             nc.vector.tensor_copy(
                 words[:].rearrange("p t (g m b) -> p g t m b", m=8, b=2),
                 raw_words[:].rearrange("p (g m t b) -> p g t m b", m=8, t=PACK, b=2),
             )
+            return words
+
+        def deal_scales(name):
+            scales = sb([P, PACK, P], U8, name)
             nc.vector.tensor_copy(
                 scales[:].rearrange("p t (g m) -> p g t m", m=16),
                 raw_scales[:].rearrange("p (g m t) -> p g t m", m=16, t=PACK),
             )
-            return words, scales
+            return scales
 
-        w1_raw_words = load_words(w1_words, "w1", nc.scalar)
-        table_scales = sb([P, T], U8, "table_scales")
-        nc.vector.memset(table_scales[:].bitcast(I32), 0)
-        nc.scalar.dma_start(table_scales[0:P:8, :].bitcast(I32), x_scales[0].bitcast(I32))
-        w1_raw = (w1_raw_words, load_scales(w1_scales, "w1", nc.vector, nc.scalar))
-
-        gain = sb([P, PACK], F32, "gain")
-        w2_raw_words = load_words(w2_words, "w2", nc.gpsimd)
+        nc.sync.dma_start(offs_t[:], offs)
+        nc.sync.dma_start(table_scales[:].bitcast(I32), x_scales[0].bitcast(I32).unsqueeze(1).to_broadcast([16, 8, T // 4]))
+        for j in range(4):
+            load_scales(w1_scales, j, nc.sync)
+        nc.sync.dma_start(w1_raw_words[:].bitcast(I32), w1_words[0].bitcast(I32))
+        nc.sync.dma_start(table_words[:].bitcast(I32), x_words[0].rearrange("p n t -> p (n t)").bitcast(I32))
+        nc.sync.dma_start(n2_t[:], n2)
+        nc.sync.dma_start(n1_t[:], n1)
+        nc.sync.dma_start(n3_t[:], n3)
         nc.gpsimd.dma_start(gain[:], gn.rearrange("(p t) o -> p (t o)", t=PACK))
-        w2_raw = (w2_raw_words, load_scales(w2_scales, "w2", nc.gpsimd, nc.gpsimd))
+        nc.gpsimd.dma_start(w2_raw_words[:].bitcast(I32), w2_words[0].bitcast(I32))
 
         x_scale = sb([P, S], U8, "x_scale")
         nc.vector.memset(x_scale[:].bitcast(I32), 0)
@@ -105,13 +101,17 @@ def tile_picked_hashsumtwice_none_po_kernel(
         for j in range(4):
             nc.sync.dma_start(x_scale[j:P:32, :].bitcast(I32), picked_rows[8 * j : P : 32, :].bitcast(I32))
 
-        w1q, w1s = deal_weight(*w1_raw, "w1")
+        w1q = deal_words(w1_raw_words, "w1q")
+        w1s = deal_scales("w1s")
+        for j in range(4):
+            load_scales(w2_scales, j, nc.sync)
 
         x_codes = sb([P, S], U32, "x_codes")
         for h0 in (0, HALF):
             nc.vector.tensor_copy(x_codes[:, h0 : h0 + HALF], table_words[:].indirect(entries(offs_t, h0, HALF)))
 
-        w2q, w2s = deal_weight(*w2_raw, "w2")
+        w2q = deal_words(w2_raw_words, "w2q")
+        w2s = deal_scales("w2s")
 
         def product(acc, wq, ws, t, codes, scales):
             nc.tensor.matmul_mx(
@@ -125,15 +125,15 @@ def tile_picked_hashsumtwice_none_po_kernel(
             )
 
         gy = [sb([P, S], F32, "gy%d" % t) for t in range(PACK)]
-        pieces = [(0, 0, HALF), (0, HALF, HALF)] + [(t, 0, S) for t in range(1, PACK)]
+        pieces = [(t, h0, HALF) for h0 in (0, HALF) for t in (0, 1)] + [(t, 0, S) for t in (2, 3)]
         for b, (t, c0, n) in enumerate(pieces):
             acc = bank(b, [P, n], "y_acc%d" % b)
             product(acc[:], w1q, w1s, t, x_codes[:, c0 : c0 + n], x_scale[:, c0 : c0 + n])
             nc.scalar.activation(gy[t][:, c0 : c0 + n], acc[:], COPY, scale=gain[:, t : t + 1])
 
         hw = [sb([P, S], F32, "hw%d" % t) for t in range(PACK)]
-        hp = [sb([P, S], F32, "hp%d" % t) for t in range(PACK)]
-        h_banks = ((5, 5, 6, 6), (7, 7, 7, 7), (0, 1, 2, 3))
+        hp = sb([P, PACK, S], F32, "hp")
+        h_banks = ((6, 6, 7, 7), (0, 1, 2, 3))
         last = len(CHUNKS) - 1
 
         def second_product(c, zb):
@@ -148,36 +148,47 @@ def tile_picked_hashsumtwice_none_po_kernel(
                 if b not in accs:
                     accs[b] = bank(b, [P, shared, n], "h_acc%d_%d" % (c, b))
                 product(accs[b][:, t % shared, :], w2q, w2s, t, zq[:], zs[:])
-            for dst in (hw, hp):
-                for t in range(PACK):
-                    b = h_banks[c][t]
-                    shared = h_banks[c].count(b)
-                    nc.scalar.activation(dst[t][:, c0 : c0 + n], accs[b][:, t % shared, :], COPY, scale=0.5)
+            for t in range(PACK):
+                b = h_banks[c][t]
+                shared = h_banks[c].count(b)
+                nc.scalar.activation(hw[t][:, c0 : c0 + n], accs[b][:, t % shared, :], COPY, scale=0.5)
+                if t % shared == shared - 1:
+                    nc.scalar.activation(hp[:, t + 1 - shared : t + 1, c0 : c0 + n], accs[b][:], COPY, scale=0.5)
 
-        waiting = None
-        for c, (c0, n) in enumerate(CHUNKS):
-            part = sb([P, PACK, n], F32, "part%d" % c)
-            z = sb([P, PACK, n], F32, "z%d" % c)
-            zb = sb([P, n, PACK], BF16, "zb%d" % c)
-            for t in range(PACK + 1):
-                if t < PACK:
-                    nc.vector.tensor_scalar(part[:, t, :], gy[t][:].indirect(entries(n2_t, c0, n)), 0.75, 0.0, MULT, ADD)
-                if t > 0:
-                    nc.vector.tensor_tensor(z[:, t - 1, :], gy[t - 1][:].indirect(entries(n1_t, c0, n)), part[:, t - 1, :], ADD)
-            if waiting is not None:
-                second_product(*waiting)
-            interleave(nc.vector.tensor_copy if c == last else nc.scalar.copy, zb, z)
-            waiting = (c, zb)
-        second_product(*waiting)
+        z = [sb([P, PACK, HALF], F32, "z%d" % c) for c in range(2)]
+        steps = [(c, t) for c in range(2) for t in range(PACK)]
+        parts = []
+        for k in range(len(steps) + 1):
+            if k == len(steps) - 1:
+                second_product(0, zb_first)
+            if k < len(steps):
+                c, t = steps[k]
+                if k == len(steps) - 1:
+                    part = keep.tile([P, HALF], F32, name="part_last", tag="zb_first", align_bytes=64)
+                else:
+                    part = ring.tile([P, HALF], F32, name="part", align_bytes=64)
+                nc.vector.tensor_scalar(part[:], gy[t][:].indirect(entries(n2_t, c * HALF, HALF)), 0.75, 0.0, MULT, ADD)
+                parts.append(part)
+            if k > 0:
+                c, t = steps[k - 1]
+                nc.vector.tensor_tensor(z[c][:, t, :], gy[t][:].indirect(entries(n1_t, c * HALF, HALF)), parts[k - 1][:], ADD)
+            if k == PACK:
+                zb_first = sb([P, HALF, PACK], BF16, "zb_first")
+                interleave(nc.scalar.copy, zb_first, z[0])
+        zb_second = sb([P, HALF, PACK], BF16, "zb_second")
+        interleave(nc.vector.tensor_copy, zb_second, z[1])
+        second_product(1, zb_second)
 
         w = [sb([P, S], F32, "w%d" % t) for t in range(PACK)]
         d = [sb([P, S], F32, "d%d" % t) for t in range(PACK)]
         for t in range(PACK):
             for h0 in (0, HALF):
                 nc.vector.tensor_tensor(
-                    w[t][:, h0 : h0 + HALF], hw[t][:].indirect(entries(n3_t, h0, HALF)), hp[t][:, h0 : h0 + HALF], SUB
+                    w[t][:, h0 : h0 + HALF], hw[t][:].indirect(entries(n3_t, h0, HALF)), hp[:, t, h0 : h0 + HALF], SUB
                 )
-            nc.scalar.activation(d[t][:], w[t][:], COPY, scale=2.0)
+        for h0 in (0, HALF):
+            for t in range(PACK):
+                nc.scalar.activation(d[t][:, h0 : h0 + HALF], w[t][:, h0 : h0 + HALF], COPY, scale=2.0)
 
         out_rows = out_0.rearrange("(p t) j -> p t j", t=PACK)
         out_words = out_1[0].rearrange("p n t -> p (n t)").bitcast(I32)
@@ -191,18 +202,20 @@ def tile_picked_hashsumtwice_none_po_kernel(
             )
             nc.sync.dma_start(out_words[:, c0 : c0 + n], oq[:].bitcast(I32))
 
-        waiting = None
+        obs = []
         for c, (c0, n) in enumerate(CHUNKS):
             o = sb([P, PACK, n], F32, "o%d" % c)
             ob = sb([P, n, PACK], BF16, "ob%d" % c)
             for t in range(PACK):
                 nc.vector.tensor_tensor(o[:, t, :], w[t][:].indirect(entries(n3_t, c0, n)), d[t][:, c0 : c0 + n], SUB)
-            nc.sync.dma_start(out_rows[:, :, c0 : c0 + n], o[:])
-            if waiting is not None:
-                planes(*waiting)
+                if c == last:
+                    nc.sync.dma_start(out_rows[:, t, c0 : c0 + n], o[:, t, :])
+            if c < last:
+                nc.sync.dma_start(out_rows[:, :, c0 : c0 + n], o[:])
             interleave(nc.vector.tensor_copy if c == last else nc.scalar.copy, ob, o)
-            waiting = (c, ob)
-        planes(*waiting)
+            obs.append(ob)
+        for c, ob in enumerate(obs):
+            planes(c, ob)
         for q in range(4):
             queue = nc.scalar if q % 2 == 0 else nc.sync
             queue.dma_start(out_2[0, 4 * q : 4 * q + 4, :].bitcast(I32), o_scale[32 * q : 32 * q + 4, :].bitcast(I32))

@@ -21,7 +21,7 @@ SUB = mybir.AluOpType.subtract
 P = 128
 PACK = 4
 HALF = S // 2
-CHUNKS = ((0, HALF), (HALF, HALF))
+QUARTER = S // 4
 
 
 def entries(lists, start, width):
@@ -30,8 +30,8 @@ def entries(lists, start, width):
 
 def interleave(engine_copy, dst, src):
     engine_copy(
-        dst[:].rearrange("p (c i) t -> p c t i", i=4),
-        src[:].rearrange("p t (c i) -> p c t i", i=4),
+        dst.rearrange("p (c i) t -> p c t i", i=4),
+        src.rearrange("p t (c i) -> p c t i", i=4),
     )
 
 
@@ -41,7 +41,7 @@ def tile_picked_hashsumtwice_none_po_kernel(
     nc = tc.nc
     with ExitStack() as ctx:
         keep = ctx.enter_context(tc.tile_pool(name="keep", bufs=1))
-        ring = ctx.enter_context(tc.tile_pool(name="ring", bufs=3))
+        ring = ctx.enter_context(tc.tile_pool(name="ring", bufs=2))
         psum = ctx.enter_context(tc.psum_pool(name="psum", bufs=1))
 
         def sb(shape, dtype, name):
@@ -82,8 +82,8 @@ def tile_picked_hashsumtwice_none_po_kernel(
             )
             return scales
 
-        nc.sync.dma_start(offs_t[:], offs)
         nc.sync.dma_start(table_scales[:].bitcast(I32), x_scales[0].bitcast(I32).unsqueeze(1).to_broadcast([16, 8, T // 4]))
+        nc.sync.dma_start(offs_t[:], offs)
         for j in range(4):
             load_scales(w1_scales, j, nc.sync)
         nc.sync.dma_start(w1_raw_words[:].bitcast(I32), w1_words[0].bitcast(I32))
@@ -124,60 +124,91 @@ def tile_picked_hashsumtwice_none_po_kernel(
                 stop=True,
             )
 
+        def quantize(codes, scales, grouped):
+            nc.vector.quantize_mx(out=codes.bitcast(FP8X4), scales=scales, in_=grouped.rearrange("p c t -> p (c t)"))
+
         gy = [sb([P, S], F32, "gy%d" % t) for t in range(PACK)]
-        pieces = [(t, h0, HALF) for h0 in (0, HALF) for t in (0, 1)] + [(t, 0, S) for t in (2, 3)]
-        for b, (t, c0, n) in enumerate(pieces):
-            acc = bank(b, [P, n], "y_acc%d" % b)
-            product(acc[:], w1q, w1s, t, x_codes[:, c0 : c0 + n], x_scale[:, c0 : c0 + n])
-            nc.scalar.activation(gy[t][:, c0 : c0 + n], acc[:], COPY, scale=gain[:, t : t + 1])
+
+        def first_product(acc, t, h0):
+            product(acc, w1q, w1s, t, x_codes[:, h0 : h0 + HALF], x_scale[:, h0 : h0 + HALF])
+
+        def gain_into_window(acc, t, h0):
+            nc.scalar.activation(gy[t][:, h0 : h0 + HALF], acc, COPY, scale=gain[:, t : t + 1])
+
+        for half, h0 in enumerate((0, HALF)):
+            for t in (0, 1):
+                acc = bank(2 * half + t, [P, HALF], "y_acc")
+                first_product(acc[:], t, h0)
+                gain_into_window(acc[:], t, h0)
+        for half, h0 in enumerate((0, HALF)):
+            acc = bank(4 + half, [P, 2, HALF], "y_acc")
+            for t in (2, 3):
+                first_product(acc[:, t - 2, :], t, h0)
+            for t in (2, 3):
+                gain_into_window(acc[:, t - 2, :], t, h0)
 
         hw = [sb([P, S], F32, "hw%d" % t) for t in range(PACK)]
         hp = sb([P, PACK, S], F32, "hp")
-        h_banks = ((6, 6, 7, 7), (0, 1, 2, 3))
-        last = len(CHUNKS) - 1
+        z = [sb([P, PACK, HALF], F32, "z%d" % half) for half in range(2)]
+        zq = sb([P, S], U32, "zq")
+        zs = sb([P, S], U8, "zs")
 
-        def second_product(c, zb):
-            c0, n = CHUNKS[c]
-            zq = sb([P, n], U32, "zq%d" % c)
-            zs = sb([P, n], U8, "zs%d" % c)
-            nc.vector.quantize_mx(out=zq[:].bitcast(FP8X4), scales=zs[:], in_=zb[:].rearrange("p c t -> p (c t)"))
-            accs = {}
-            for t in range(PACK):
-                b = h_banks[c][t]
-                shared = h_banks[c].count(b)
-                if b not in accs:
-                    accs[b] = bank(b, [P, shared, n], "h_acc%d_%d" % (c, b))
-                product(accs[b][:, t % shared, :], w2q, w2s, t, zq[:], zs[:])
-            for t in range(PACK):
-                b = h_banks[c][t]
-                shared = h_banks[c].count(b)
-                nc.scalar.activation(hw[t][:, c0 : c0 + n], accs[b][:, t % shared, :], COPY, scale=0.5)
-                if t % shared == shared - 1:
-                    nc.scalar.activation(hp[:, t + 1 - shared : t + 1, c0 : c0 + n], accs[b][:], COPY, scale=0.5)
+        def three_quarters(part, t, h0):
+            nc.vector.tensor_scalar(part[:], gy[t][:].indirect(entries(n2_t, h0, HALF)), 0.75, 0.0, MULT, ADD)
 
-        z = [sb([P, PACK, HALF], F32, "z%d" % c) for c in range(2)]
-        steps = [(c, t) for c in range(2) for t in range(PACK)]
-        parts = []
-        for k in range(len(steps) + 1):
-            if k == len(steps) - 1:
-                second_product(0, zb_first)
-            if k < len(steps):
-                c, t = steps[k]
-                if k == len(steps) - 1:
-                    part = keep.tile([P, HALF], F32, name="part_last", tag="zb_first", align_bytes=64)
+        def add_first(half, t, part, c0, n):
+            nc.vector.tensor_tensor(
+                z[half][:, t, c0 : c0 + n], gy[t][:].indirect(entries(n1_t, half * HALF + c0, n)), part[:, c0 : c0 + n], ADD
+            )
+
+        def second_product_first_half():
+            quantize(zq[:, 0:HALF], zs[:, 0:HALF], zb_first[:])
+            for pair in range(2):
+                acc = bank(6 + pair, [P, 2, HALF], "h_acc")
+                for u in range(2):
+                    product(acc[:, u, :], w2q, w2s, 2 * pair + u, zq[:, 0:HALF], zs[:, 0:HALF])
+                for u in range(2):
+                    nc.scalar.activation(hw[2 * pair + u][:, 0:HALF], acc[:, u, :], COPY, scale=0.5)
+                nc.scalar.activation(hp[:, 2 * pair : 2 * pair + 2, 0:HALF], acc[:], COPY, scale=0.5)
+
+        for half in range(2):
+            for t in (0, 2):
+                part_a = ring.tile([P, HALF], F32, name="part", align_bytes=64)
+                three_quarters(part_a, t, half * HALF)
+                if (half, t) == (1, 2):
+                    second_product_first_half()
+                    part_b = keep.tile([P, HALF], F32, name="part_last", tag="zb_first", align_bytes=64)
                 else:
-                    part = ring.tile([P, HALF], F32, name="part", align_bytes=64)
-                nc.vector.tensor_scalar(part[:], gy[t][:].indirect(entries(n2_t, c * HALF, HALF)), 0.75, 0.0, MULT, ADD)
-                parts.append(part)
-            if k > 0:
-                c, t = steps[k - 1]
-                nc.vector.tensor_tensor(z[c][:, t, :], gy[t][:].indirect(entries(n1_t, c * HALF, HALF)), parts[k - 1][:], ADD)
-            if k == PACK:
+                    part_b = ring.tile([P, HALF], F32, name="part", align_bytes=64)
+                three_quarters(part_b, t + 1, half * HALF)
+                add_first(half, t, part_a, 0, HALF)
+                if (half, t) == (1, 2):
+                    add_first(half, t + 1, part_b, 0, QUARTER)
+                    add_first(half, t + 1, part_b, QUARTER, QUARTER)
+                else:
+                    add_first(half, t + 1, part_b, 0, HALF)
+            if half == 0:
                 zb_first = sb([P, HALF, PACK], BF16, "zb_first")
-                interleave(nc.scalar.copy, zb_first, z[0])
-        zb_second = sb([P, HALF, PACK], BF16, "zb_second")
-        interleave(nc.vector.tensor_copy, zb_second, z[1])
-        second_product(1, zb_second)
+                interleave(nc.scalar.copy, zb_first[:], z[0][:])
+
+        zb_late = [sb([P, QUARTER, PACK], BF16, "zb_late%d" % i) for i in range(2)]
+        for i in range(2):
+            interleave(nc.vector.tensor_copy, zb_late[i][:], z[1][:, :, i * QUARTER : (i + 1) * QUARTER])
+        for i in range(2):
+            c0 = HALF + i * QUARTER
+            quantize(zq[:, c0 : c0 + QUARTER], zs[:, c0 : c0 + QUARTER], zb_late[i][:])
+        late = [(0, HALF, QUARTER), (0, HALF + QUARTER, QUARTER)] + [(t, HALF, HALF) for t in range(1, PACK)]
+        late_accs = []
+        for b, (t, c0, n) in enumerate(late):
+            acc = bank(b, [P, n], "h_acc")
+            product(acc[:], w2q, w2s, t, zq[:, c0 : c0 + n], zs[:, c0 : c0 + n])
+            late_accs.append(acc)
+        for t in range(PACK):
+            mine = [(acc, c0, n) for acc, (u, c0, n) in zip(late_accs, late) if u == t]
+            for acc, c0, n in mine:
+                nc.scalar.activation(hw[t][:, c0 : c0 + n], acc[:], COPY, scale=0.5)
+            for acc, c0, n in mine:
+                nc.scalar.activation(hp[:, t, c0 : c0 + n], acc[:], COPY, scale=0.5)
 
         w = [sb([P, S], F32, "w%d" % t) for t in range(PACK)]
         d = [sb([P, S], F32, "d%d" % t) for t in range(PACK)]
@@ -192,30 +223,35 @@ def tile_picked_hashsumtwice_none_po_kernel(
 
         out_rows = out_0.rearrange("(p t) j -> p t j", t=PACK)
         out_words = out_1[0].rearrange("p n t -> p (n t)").bitcast(I32)
+        o = [sb([P, PACK, HALF], F32, "o%d" % half) for half in range(2)]
+        oq = [sb([P, HALF], U32, "oq%d" % half) for half in range(2)]
         o_scale = sb([P, S], U8, "o_scale")
 
-        def planes(c, ob):
-            c0, n = CHUNKS[c]
-            oq = sb([P, n], U32, "oq%d" % c)
-            nc.vector.quantize_mx(
-                out=oq[:].bitcast(FP8X4), scales=o_scale[:, c0 : c0 + n], in_=ob[:].rearrange("p c t -> p (c t)")
-            )
-            nc.sync.dma_start(out_words[:, c0 : c0 + n], oq[:].bitcast(I32))
+        def result(half, t, c0, n):
+            j0 = half * HALF + c0
+            nc.vector.tensor_tensor(o[half][:, t, c0 : c0 + n], w[t][:].indirect(entries(n3_t, j0, n)), d[t][:, j0 : j0 + n], SUB)
 
-        obs = []
-        for c, (c0, n) in enumerate(CHUNKS):
-            o = sb([P, PACK, n], F32, "o%d" % c)
-            ob = sb([P, n, PACK], BF16, "ob%d" % c)
-            for t in range(PACK):
-                nc.vector.tensor_tensor(o[:, t, :], w[t][:].indirect(entries(n3_t, c0, n)), d[t][:, c0 : c0 + n], SUB)
-                if c == last:
-                    nc.sync.dma_start(out_rows[:, t, c0 : c0 + n], o[:, t, :])
-            if c < last:
-                nc.sync.dma_start(out_rows[:, :, c0 : c0 + n], o[:])
-            interleave(nc.vector.tensor_copy if c == last else nc.scalar.copy, ob, o)
-            obs.append(ob)
-        for c, ob in enumerate(obs):
-            planes(c, ob)
+        for t in range(PACK):
+            result(0, t, 0, HALF)
+        nc.sync.dma_start(out_rows[:, :, 0:HALF], o[0][:])
+        ob_first = sb([P, HALF, PACK], BF16, "ob_first")
+        interleave(nc.scalar.copy, ob_first[:], o[0][:])
+        for t in range(PACK):
+            if t < PACK - 1:
+                result(1, t, 0, HALF)
+            else:
+                result(1, t, 0, QUARTER)
+                result(1, t, QUARTER, QUARTER)
+            nc.sync.dma_start(out_rows[:, t, HALF:S], o[1][:, t, :])
+        ob_late = [sb([P, QUARTER, PACK], BF16, "ob_late%d" % i) for i in range(2)]
+        for i in range(2):
+            interleave(nc.vector.tensor_copy, ob_late[i][:], o[1][:, :, i * QUARTER : (i + 1) * QUARTER])
+        quantize(oq[0][:], o_scale[:, 0:HALF], ob_first[:])
+        nc.sync.dma_start(out_words[:, 0:HALF], oq[0][:].bitcast(I32))
+        for i in range(2):
+            c0 = i * QUARTER
+            quantize(oq[1][:, c0 : c0 + QUARTER], o_scale[:, HALF + c0 : HALF + c0 + QUARTER], ob_late[i][:])
+        nc.sync.dma_start(out_words[:, HALF:S], oq[1][:].bitcast(I32))
         for q in range(4):
             queue = nc.scalar if q % 2 == 0 else nc.sync
             queue.dma_start(out_2[0, 4 * q : 4 * q + 4, :].bitcast(I32), o_scale[32 * q : 32 * q + 4, :].bitcast(I32))

@@ -62,9 +62,9 @@ def tile_picked_hashsumtwice_none_po_kernel(
         w1_raw_words = sb([P, 2 * H], U8, "w1_raw_words")
         w2_raw_words = sb([P, 2 * H], U8, "w2_raw_words")
 
-        def load_scales(scales, j, queue):
-            rows = scales[0].bitcast(I32).rearrange("(q j) c -> j q c", j=4)[j]
-            queue.dma_start(raw_scales[j:P:4, :].bitcast(I32), rows.unsqueeze(1).to_broadcast([4, 8, H // 4]))
+        def load_scales(scales, queue):
+            for q in range(4):
+                queue.dma_start(raw_scales[32 * q : 32 * q + 4, :].bitcast(I32), scales[0, 4 * q : 4 * q + 4, :].bitcast(I32))
 
         def deal_words(raw_words, name):
             words = sb([P, PACK, 2 * P], U8, name)
@@ -84,13 +84,11 @@ def tile_picked_hashsumtwice_none_po_kernel(
 
         nc.sync.dma_start(table_scales[:].bitcast(I32), x_scales[0].bitcast(I32).unsqueeze(1).to_broadcast([16, 8, T // 4]))
         nc.sync.dma_start(offs_t[:], offs)
-        for j in range(4):
-            load_scales(w1_scales, j, nc.sync)
+        nc.gpsimd.memset(raw_scales[:].bitcast(I32), 0)
+        load_scales(w1_scales, nc.scalar)
         nc.sync.dma_start(w1_raw_words[:].bitcast(I32), w1_words[0].bitcast(I32))
         nc.sync.dma_start(table_words[:].bitcast(I32), x_words[0].rearrange("p n t -> p (n t)").bitcast(I32))
         nc.sync.dma_start(n2_t[:], n2)
-        nc.sync.dma_start(n1_t[:], n1)
-        nc.sync.dma_start(n3_t[:], n3)
         nc.gpsimd.dma_start(gain[:], gn.rearrange("(p t) o -> p (t o)", t=PACK))
         nc.gpsimd.dma_start(w2_raw_words[:].bitcast(I32), w2_words[0].bitcast(I32))
 
@@ -99,12 +97,14 @@ def tile_picked_hashsumtwice_none_po_kernel(
         picked_rows = sb([P, S], U8, "picked_rows")
         nc.vector.tensor_copy(picked_rows[:], table_scales[:].indirect(offs_t[:]))
         for j in range(4):
-            nc.sync.dma_start(x_scale[j:P:32, :].bitcast(I32), picked_rows[8 * j : P : 32, :].bitcast(I32))
+            queue = nc.sync if j % 2 == 0 else nc.scalar
+            queue.dma_start(x_scale[j:P:32, :].bitcast(I32), picked_rows[8 * j : P : 32, :].bitcast(I32))
+        nc.sync.dma_start(n1_t[:], n1)
+        nc.sync.dma_start(n3_t[:], n3)
 
         w1q = deal_words(w1_raw_words, "w1q")
         w1s = deal_scales("w1s")
-        for j in range(4):
-            load_scales(w2_scales, j, nc.sync)
+        load_scales(w2_scales, nc.sync)
 
         x_codes = sb([P, S], U32, "x_codes")
         for h0 in (0, HALF):
@@ -243,11 +243,13 @@ def tile_picked_hashsumtwice_none_po_kernel(
                 result(1, t, 0, QUARTER)
                 result(1, t, QUARTER, QUARTER)
             nc.sync.dma_start(out_rows[:, t, HALF:S], o[1][:, t, :])
-        ob_late = [sb([P, QUARTER, PACK], BF16, "ob_late%d" % i) for i in range(2)]
-        for i in range(2):
-            interleave(nc.vector.tensor_copy, ob_late[i][:], o[1][:, :, i * QUARTER : (i + 1) * QUARTER])
+        ob_third = sb([P, QUARTER, PACK], BF16, "ob_third")
+        interleave(nc.scalar.copy, ob_third[:], o[1][:, :, 0:QUARTER])
         quantize(oq[0][:], o_scale[:, 0:HALF], ob_first[:])
         nc.sync.dma_start(out_words[:, 0:HALF], oq[0][:].bitcast(I32))
+        ob_fourth = keep.tile([P, QUARTER, PACK], BF16, name="ob_fourth", tag="ob_first", align_bytes=64)
+        interleave(nc.vector.tensor_copy, ob_fourth[:], o[1][:, :, QUARTER:HALF])
+        ob_late = [ob_third, ob_fourth]
         for i in range(2):
             c0 = i * QUARTER
             quantize(oq[1][:, c0 : c0 + QUARTER], o_scale[:, HALF + c0 : HALF + c0 + QUARTER], ob_late[i][:])

from contextlib import ExitStack

import concourse.mybir as mybir

K, T, S, N, H = 512, 2048, 512, 512, 512
FLOPS = 2 * K * H * S + 2 * H * N * S

F32 = mybir.dt.float32
BF16 = mybir.dt.bfloat16
I32 = mybir.dt.int32
U32 = mybir.dt.uint32
U16 = mybir.dt.uint16
U8 = mybir.dt.uint8
FP8X4 = mybir.dt.float8_e4m3fn_x4
FP4X4 = mybir.dt.float4_e2m1fn_x4
COPY = mybir.ActivationFunctionType.Copy
MULT = mybir.AluOpType.mult
ADD = mybir.AluOpType.add
SUB = mybir.AluOpType.subtract

P = 128
PACK = 4
HALF = S // 2
QUARTER = S // 4


def entries(lists, start, width):
    return lists[:, start // 16 : (start + width) // 16]


def interleave(engine_copy, dst, src):
    engine_copy(
        dst.rearrange("p (c i) t -> p c t i", i=4),
        src.rearrange("p t (c i) -> p c t i", i=4),
    )


def tile_picked_hashsumtwice_none_po_kernel(
    tc, x_words, x_scales, w1_words, w1_scales, gn, w2_words, w2_scales, offs, n1, n2, n3, out_0, out_1, out_2
):
    nc = tc.nc
    with ExitStack() as ctx:
        keep = ctx.enter_context(tc.tile_pool(name="keep", bufs=1))
        ring = ctx.enter_context(tc.tile_pool(name="ring", bufs=2))
        psum = ctx.enter_context(tc.psum_pool(name="psum", bufs=1))

        def sb(shape, dtype, name):
            return keep.tile(shape, dtype, name=name, align_bytes=64)

        def bank(index, shape, name):
            return psum.tile(shape, F32, name=name, tag="bank%d" % index)

        offs_t = keep.tile([P, S // 16], U16, name="offs_t")
        n1_t = keep.tile([P, S // 16], U16, name="n1_t")
        n2_t = keep.tile([P, S // 16], U16, name="n2_t")
        n3_t = keep.tile([P, S // 16], U16, name="n3_t")
        table_words = sb([P, T], U32, "table_words")
        table_scales = sb([P, T], U8, "table_scales")
        gain = sb([P, PACK], F32, "gain")

        raw_scales = sb([P, H], U8, "raw_scales")
        w1_raw_words = sb([P, 2 * H], U8, "w1_raw_words")
        w2_raw_words = sb([P, 2 * H], U8, "w2_raw_words")

        def load_scales(scales, queue):
            for q in range(4):
                queue.dma_start(raw_scales[32 * q : 32 * q + 4, :].bitcast(I32), scales[0, 4 * q : 4 * q + 4, :].bitcast(I32))

        def deal_words(raw_words, name):
            words = sb([P, PACK, 2 * P], U8, name)
            nc.vector.tensor_copy(
                words[:].rearrange("p t (g m b) -> p g t m b", m=8, b=2),
                raw_words[:].rearrange("p (g m t b) -> p g t m b", m=8, t=PACK, b=2),
            )
            return words

        def deal_scales(name):
            scales = sb([P, PACK, P], U8, name)
            nc.vector.tensor_copy(
                scales[:].rearrange("p t (g m) -> p g t m", m=16),
                raw_scales[:].rearrange("p (g m t) -> p g t m", m=16, t=PACK),
            )
            return scales

        nc.sync.dma_start(table_scales[:].bitcast(I32), x_scales[0].bitcast(I32).unsqueeze(1).to_broadcast([16, 8, T // 4]))
        nc.sync.dma_start(offs_t[:], offs)
        nc.gpsimd.memset(raw_scales[:].bitcast(I32), 0)
        load_scales(w1_scales, nc.scalar)
        nc.sync.dma_start(w1_raw_words[:].bitcast(I32), w1_words[0].bitcast(I32))
        nc.sync.dma_start(table_words[:].bitcast(I32), x_words[0].rearrange("p n t -> p (n t)").bitcast(I32))
        nc.sync.dma_start(n2_t[:], n2)
        nc.gpsimd.dma_start(gain[:], gn.rearrange("(p t) o -> p (t o)", t=PACK))
        nc.gpsimd.dma_start(w2_raw_words[:].bitcast(I32), w2_words[0].bitcast(I32))

        x_scale = sb([P, S], U8, "x_scale")
        nc.vector.memset(x_scale[:].bitcast(I32), 0)
        picked_rows = sb([P, S], U8, "picked_rows")
        nc.vector.tensor_copy(picked_rows[:], table_scales[:].indirect(offs_t[:]))
        for j in range(4):
            queue = nc.sync if j % 2 == 0 else nc.scalar
            queue.dma_start(x_scale[j:P:32, :].bitcast(I32), picked_rows[8 * j : P : 32, :].bitcast(I32))
        nc.sync.dma_start(n1_t[:], n1)
        nc.sync.dma_start(n3_t[:], n3)

        w1q = deal_words(w1_raw_words, "w1q")
        w1s = deal_scales("w1s")
        load_scales(w2_scales, nc.sync)

        x_codes = sb([P, S], U32, "x_codes")
        for h0 in (0, HALF):
            nc.vector.tensor_copy(x_codes[:, h0 : h0 + HALF], table_words[:].indirect(entries(offs_t, h0, HALF)))

        w2q = deal_words(w2_raw_words, "w2q")
        w2s = deal_scales("w2s")

        def product(acc, wq, ws, t, codes, scales):
            nc.tensor.matmul_mx(
                out=acc,
                lhsT=wq[:, t, :].bitcast(FP4X4),
                lhsT_scale=ws[:, t, :],
                rhs=codes.bitcast(FP8X4),
                rhs_scale=scales,
                start=True,
                stop=True,
            )

        def quantize(codes, scales, grouped):
            nc.vector.quantize_mx(out=codes.bitcast(FP8X4), scales=scales, in_=grouped.rearrange("p c t -> p (c t)"))

        gy = [sb([P, S], F32, "gy%d" % t) for t in range(PACK)]

        def first_product(acc, t, h0):
            product(acc, w1q, w1s, t, x_codes[:, h0 : h0 + HALF], x_scale[:, h0 : h0 + HALF])

        def gain_into_window(acc, t, h0):
            nc.scalar.activation(gy[t][:, h0 : h0 + HALF], acc, COPY, scale=gain[:, t : t + 1])

        for half, h0 in enumerate((0, HALF)):
            for t in (0, 1):
                acc = bank(2 * half + t, [P, HALF], "y_acc")
                first_product(acc[:], t, h0)
                gain_into_window(acc[:], t, h0)
        for half, h0 in enumerate((0, HALF)):
            acc = bank(4 + half, [P, 2, HALF], "y_acc")
            for t in (2, 3):
                first_product(acc[:, t - 2, :], t, h0)
            for t in (2, 3):
                gain_into_window(acc[:, t - 2, :], t, h0)

        hw = [sb([P, S], F32, "hw%d" % t) for t in range(PACK)]
        hp = sb([P, PACK, S], F32, "hp")
        z = [sb([P, PACK, HALF], F32, "z%d" % half) for half in range(2)]
        zq = sb([P, S], U32, "zq")
        zs = sb([P, S], U8, "zs")

        def three_quarters(part, t, h0):
            nc.vector.tensor_scalar(part[:], gy[t][:].indirect(entries(n2_t, h0, HALF)), 0.75, 0.0, MULT, ADD)

        def add_first(half, t, part, c0, n):
            nc.vector.tensor_tensor(
                z[half][:, t, c0 : c0 + n], gy[t][:].indirect(entries(n1_t, half * HALF + c0, n)), part[:, c0 : c0 + n], ADD
            )

        def second_product_first_half():
            quantize(zq[:, 0:HALF], zs[:, 0:HALF], zb_first[:])
            for pair in range(2):
                acc = bank(6 + pair, [P, 2, HALF], "h_acc")
                for u in range(2):
                    product(acc[:, u, :], w2q, w2s, 2 * pair + u, zq[:, 0:HALF], zs[:, 0:HALF])
                for u in range(2):
                    nc.scalar.activation(hw[2 * pair + u][:, 0:HALF], acc[:, u, :], COPY, scale=0.5)
                nc.scalar.activation(hp[:, 2 * pair : 2 * pair + 2, 0:HALF], acc[:], COPY, scale=0.5)

        for half in range(2):
            for t in (0, 2):
                part_a = ring.tile([P, HALF], F32, name="part", align_bytes=64)
                three_quarters(part_a, t, half * HALF)
                if (half, t) == (1, 2):
                    second_product_first_half()
                    part_b = keep.tile([P, HALF], F32, name="part_last", tag="zb_first", align_bytes=64)
                else:
                    part_b = ring.tile([P, HALF], F32, name="part", align_bytes=64)
                three_quarters(part_b, t + 1, half * HALF)
                add_first(half, t, part_a, 0, HALF)
                if (half, t) == (1, 2):
                    add_first(half, t + 1, part_b, 0, QUARTER)
                    add_first(half, t + 1, part_b, QUARTER, QUARTER)
                else:
                    add_first(half, t + 1, part_b, 0, HALF)
            if half == 0:
                zb_first = sb([P, HALF, PACK], BF16, "zb_first")
                interleave(nc.scalar.copy, zb_first[:], z[0][:])

        zb_late = [sb([P, QUARTER, PACK], BF16, "zb_late%d" % i) for i in range(2)]
        for i in range(2):
            interleave(nc.vector.tensor_copy, zb_late[i][:], z[1][:, :, i * QUARTER : (i + 1) * QUARTER])
        for i in range(2):
            c0 = HALF + i * QUARTER
            quantize(zq[:, c0 : c0 + QUARTER], zs[:, c0 : c0 + QUARTER], zb_late[i][:])
        late = [(0, HALF, QUARTER), (0, HALF + QUARTER, QUARTER)] + [(t, HALF, HALF) for t in range(1, PACK)]
        late_accs = []
        for b, (t, c0, n) in enumerate(late):
            acc = bank(b, [P, n], "h_acc")
            product(acc[:], w2q, w2s, t, zq[:, c0 : c0 + n], zs[:, c0 : c0 + n])
            late_accs.append(acc)
        for t in range(PACK):
            mine = [(acc, c0, n) for acc, (u, c0, n) in zip(late_accs, late) if u == t]
            for acc, c0, n in mine:
                nc.scalar.activation(hw[t][:, c0 : c0 + n], acc[:], COPY, scale=0.5)
            for acc, c0, n in mine:
                nc.scalar.activation(hp[:, t, c0 : c0 + n], acc[:], COPY, scale=0.5)

        w = [sb([P, S], F32, "w%d" % t) for t in range(PACK)]
        d = [sb([P, S], F32, "d%d" % t) for t in range(PACK)]
        for t in range(PACK):
            for h0 in (0, HALF):
                nc.vector.tensor_tensor(
                    w[t][:, h0 : h0 + HALF], hw[t][:].indirect(entries(n3_t, h0, HALF)), hp[:, t, h0 : h0 + HALF], SUB
                )
        for h0 in (0, HALF):
            for t in range(PACK):
                nc.scalar.activation(d[t][:, h0 : h0 + HALF], w[t][:, h0 : h0 + HALF], COPY, scale=2.0)

        out_rows = out_0.rearrange("(p t) j -> p t j", t=PACK)
        out_words = out_1[0].rearrange("p n t -> p (n t)").bitcast(I32)
        o = [sb([P, PACK, HALF], F32, "o%d" % half) for half in range(2)]
        oq = [sb([P, HALF], U32, "oq%d" % half) for half in range(2)]
        o_scale = sb([P, S], U8, "o_scale")

        def result(half, t, c0, n):
            j0 = half * HALF + c0
            nc.vector.tensor_tensor(o[half][:, t, c0 : c0 + n], w[t][:].indirect(entries(n3_t, j0, n)), d[t][:, j0 : j0 + n], SUB)

        for t in range(PACK):
            result(0, t, 0, HALF)
        nc.sync.dma_start(out_rows[:, :, 0:HALF], o[0][:])
        ob_first = sb([P, HALF, PACK], BF16, "ob_first")
        interleave(nc.scalar.copy, ob_first[:], o[0][:])
        for t in range(PACK):
            if t < PACK - 1:
                result(1, t, 0, HALF)
            else:
                result(1, t, 0, QUARTER)
                result(1, t, QUARTER, QUARTER)
            nc.sync.dma_start(out_rows[:, t, HALF:S], o[1][:, t, :])
        ob_third = sb([P, QUARTER, PACK], BF16, "ob_third")
        interleave(nc.scalar.copy, ob_third[:], o[1][:, :, 0:QUARTER])
        quantize(oq[0][:], o_scale[:, 0:HALF], ob_first[:])
        nc.sync.dma_start(out_words[:, 0:HALF], oq[0][:].bitcast(I32))
        ob_fourth = keep.tile([P, QUARTER, PACK], BF16, name="ob_fourth", tag="ob_first", align_bytes=64)
        interleave(nc.vector.tensor_copy, ob_fourth[:], o[1][:, :, QUARTER:HALF])
        ob_late = [ob_third, ob_fourth]
        for i in range(2):
            c0 = i * QUARTER
            quantize(oq[1][:, c0 : c0 + QUARTER], o_scale[:, HALF + c0 : HALF + c0 + QUARTER], ob_late[i][:])
        nc.sync.dma_start(out_words[:, HALF:S], oq[1][:].bitcast(I32))
        for q in range(4):
            queue = nc.scalar if q % 2 == 0 else nc.sync
            queue.dma_start(out_2[0, 4 * q : 4 * q + 4, :].bitcast(I32), o_scale[32 * q : 32 * q + 4, :].bitcast(I32))
